import numpy as np
CORES = [4,20,36,52,68,84,100,116,12,28,44,60,76,92,108,124]
N = 16
def setup_inputs(rng):
    return {"x": rng.standard_normal((N, 128, 16), dtype=np.float32)}
def reference(x):
    s = (x.sum(axis=0, dtype=np.float64) / N).astype(x.dtype)
    b = 16 // N
    return {"y": np.stack([s[:, r * b:(r + 1) * b] for r in range(N)])}

@@ -1,0 +1,64 @@
+from concourse.bass import DstId, RemoteDMATransfer
+from concourse.mybir import AluOpType
+
+SCRATCH = {
+    "land": ("sbuf", [128, 32], "float32"),
+    "cst": ("sbuf", [128, 4], "float32"),
+    "tmp": ("sbuf", [128, 4], "float32"),
+    "out": ("sbuf", [128, 4], "float32"),
+    "xd": ("dram", [128, 16], "float32"),
+    "gath": ("dram", [8, 128, 16], "float32"),
+}
+SEMAPHORES = ["ld", "sent", "arr1", "arr2", "c_ok", "t_ok", "o_ok", "st"]
+
+HELPER = 6
+
+
+def rank_program(g, core, T, topo):
+    S = T.sem
+    ch, k = topo.chip(core), core % 8
+    rank_on = {}
+    for c in T.cores:
+        rank_on[topo.chip(c)] = c
+    plane = sorted(c for c in rank_on if (c & 1) == (ch & 1))
+
+    def dst(c):
+        rid, pid, _se = topo.addr(c)
+        return DstId(rid=rid, pnc=pid)
+
+    rank = T.rank_of(core)
+    if rank is not None:
+        a, n = plane.index(ch), len(plane)
+        g.sync.dma_start(T.xd[:], T.x[:]).then_inc(S.ld, 16)
+        g.vector.memset(T.cst[:], 1.0 / len(T.cores)).then_inc(S.c_ok, 1)
+        tr = []
+        for d in range(1, n):
+            tr.append(RemoteDMATransfer(dst_ids=[dst(plane[(a + d) % n] * 8 + HELPER)], dma_engine_mask=1 << (d - 1),
+                                        remote_sem=S.arr1, srcs=[T.xd[:]], dsts=[T.gath[a]], alu_op=0))
+        tr.append(RemoteDMATransfer(dst_ids=[dst(ch * 8 + HELPER)], dma_engine_mask=0xFF00,
+                                    remote_sem=S.arr1, srcs=[T.xd[:]], dsts=[T.gath[a]], alu_op=0))
+        g.wait_ge(S.ld, 16)
+        g.remote_dma_fused(tr, local_sem=S.sent)
+        v = g.vector
+        v.wait_ge(S.c_ok, 1)
+        v.wait_ge(S.arr2, 16)
+        v.tensor_tensor(T.tmp[:, 0:1], T.land[:, rank:rank + 1], T.land[:, 16 + rank:17 + rank],
+                        AluOpType.add).then_inc(S.t_ok, 1)
+        v.wait_ge(S.t_ok, 1)
+        v.tensor_tensor(T.out[:, 0:1], T.tmp[:, 0:1], T.cst[:, 0:1], AluOpType.mult).then_inc(S.o_ok, 1)
+        g.sync.wait_ge(S.o_ok, 1)
+        g.sync.dma_start(T.y[:], T.out[:, 0:1]).then_inc(S.st, 16)
+        g.sync.wait_ge(S.st, 16)
+        g.wait_ge(S.sent, (n - 1) + 8)
+        return
+
+    if k == HELPER and ch in rank_on and (ch ^ 1) in rank_on:
+        n = len(plane)
+        srcs = [T.gath[s] for s in range(n)]
+        tr = [RemoteDMATransfer(dst_ids=[dst(rank_on[ch ^ 1])], dma_engine_mask=0x00FF, remote_sem=S.arr2,
+                                srcs=srcs, dsts=[T.land[:, 16:32]], alu_op=1),
+              RemoteDMATransfer(dst_ids=[dst(rank_on[ch])], dma_engine_mask=0xFF00, remote_sem=S.arr2,
+                                srcs=srcs, dsts=[T.land[:, 0:16]], alu_op=1)]
+        g.wait_ge(S.arr1, (n - 1) + 8)
+        g.remote_dma_fused(tr, local_sem=S.sent)
+        g.wait_ge(S.sent, 16)

@@ -2,16 +2,19 @@ from concourse.bass import DstId, RemoteDMATransfer
 from concourse.mybir import AluOpType
 
 SCRATCH = {
-    "land": ("sbuf", [128, 32], "float32"),
+    "land": ("sbuf", [128, 128], "float32"),
     "cst": ("sbuf", [128, 4], "float32"),
-    "tmp": ("sbuf", [128, 4], "float32"),
+    "t4": ("sbuf", [128, 4], "float32"),
+    "t2": ("sbuf", [128, 4], "float32"),
+    "t1": ("sbuf", [128, 4], "float32"),
     "out": ("sbuf", [128, 4], "float32"),
     "xd": ("dram", [128, 16], "float32"),
-    "gath": ("dram", [8, 128, 16], "float32"),
+    "gath": ("dram", [2, 128, 16], "float32"),
 }
-SEMAPHORES = ["ld", "sent", "arr1", "arr2", "c_ok", "t_ok", "o_ok", "st"]
+SEMAPHORES = ["ld", "sent", "arr1", "arr2", "c_ok", "t4_ok", "t2_ok", "t1_ok", "o_ok", "st"]
 
-HELPER = 6
+MID = [6, 7, 2, 3]
+PER = 2
 
 
 def rank_program(g, core, T, topo):
@@ -21,6 +24,7 @@ def rank_program(g, core, T, topo):
     for c in T.cores:
         rank_on[topo.chip(c)] = c
     plane = sorted(c for c in rank_on if (c & 1) == (ch & 1))
+    n = len(plane)
 
     def dst(c):
         rid, pid, _se = topo.addr(c)
@@ -28,37 +32,43 @@ def rank_program(g, core, T, topo):
 
     rank = T.rank_of(core)
     if rank is not None:
-        a, n = plane.index(ch), len(plane)
+        a = plane.index(ch)
+        mid, slot = MID[a // PER], a % PER
         g.sync.dma_start(T.xd[:], T.x[:]).then_inc(S.ld, 16)
         g.vector.memset(T.cst[:], 1.0 / len(T.cores)).then_inc(S.c_ok, 1)
         tr = []
         for d in range(1, n):
-            tr.append(RemoteDMATransfer(dst_ids=[dst(plane[(a + d) % n] * 8 + HELPER)], dma_engine_mask=1 << (d - 1),
-                                        remote_sem=S.arr1, srcs=[T.xd[:]], dsts=[T.gath[a]], alu_op=0))
-        tr.append(RemoteDMATransfer(dst_ids=[dst(ch * 8 + HELPER)], dma_engine_mask=0xFF00,
-                                    remote_sem=S.arr1, srcs=[T.xd[:]], dsts=[T.gath[a]], alu_op=0))
+            tr.append(RemoteDMATransfer(dst_ids=[dst(plane[(a + d) % n] * 8 + mid)], dma_engine_mask=1 << (d - 1),
+                                        remote_sem=S.arr1, srcs=[T.xd[:]], dsts=[T.gath[slot]], alu_op=0))
+        tr.append(RemoteDMATransfer(dst_ids=[dst(ch * 8 + mid)], dma_engine_mask=0xFF00,
+                                    remote_sem=S.arr1, srcs=[T.xd[:]], dsts=[T.gath[slot]], alu_op=0))
         g.wait_ge(S.ld, 16)
         g.remote_dma_fused(tr, local_sem=S.sent)
         v = g.vector
+        r = rank
         v.wait_ge(S.c_ok, 1)
-        v.wait_ge(S.arr2, 16)
-        v.tensor_tensor(T.tmp[:, 0:1], T.land[:, rank:rank + 1], T.land[:, 16 + rank:17 + rank],
-                        AluOpType.add).then_inc(S.t_ok, 1)
-        v.wait_ge(S.t_ok, 1)
-        v.tensor_tensor(T.out[:, 0:1], T.tmp[:, 0:1], T.cst[:, 0:1], AluOpType.mult).then_inc(S.o_ok, 1)
+        v.wait_ge(S.arr2, 8 * 2 * len(MID))
+        v.tensor_tensor(T.t4[:, 0:4], T.land[:, r:64:16], T.land[:, 64 + r:128:16], AluOpType.add).then_inc(S.t4_ok, 1)
+        v.wait_ge(S.t4_ok, 1)
+        v.tensor_tensor(T.t2[:, 0:2], T.t4[:, 0:2], T.t4[:, 2:4], AluOpType.add).then_inc(S.t2_ok, 1)
+        v.wait_ge(S.t2_ok, 1)
+        v.tensor_tensor(T.t1[:, 0:1], T.t2[:, 0:1], T.t2[:, 1:2], AluOpType.add).then_inc(S.t1_ok, 1)
+        v.wait_ge(S.t1_ok, 1)
+        v.tensor_tensor(T.out[:, 0:1], T.t1[:, 0:1], T.cst[:, 0:1], AluOpType.mult).then_inc(S.o_ok, 1)
         g.sync.wait_ge(S.o_ok, 1)
         g.sync.dma_start(T.y[:], T.out[:, 0:1]).then_inc(S.st, 16)
         g.sync.wait_ge(S.st, 16)
         g.wait_ge(S.sent, (n - 1) + 8)
         return
 
-    if k == HELPER and ch in rank_on and (ch ^ 1) in rank_on:
-        n = len(plane)
-        srcs = [T.gath[s] for s in range(n)]
+    if k in MID and ch in rank_on and (ch ^ 1) in rank_on:
+        m = MID.index(k)
+        own = plane.index(ch) // PER == m
+        srcs = [T.gath[s] for s in range(PER)]
         tr = [RemoteDMATransfer(dst_ids=[dst(rank_on[ch ^ 1])], dma_engine_mask=0x00FF, remote_sem=S.arr2,
-                                srcs=srcs, dsts=[T.land[:, 16:32]], alu_op=1),
+                                srcs=srcs, dsts=[T.land[:, 64 + 16 * m:80 + 16 * m]], alu_op=1),
               RemoteDMATransfer(dst_ids=[dst(rank_on[ch])], dma_engine_mask=0xFF00, remote_sem=S.arr2,
-                                srcs=srcs, dsts=[T.land[:, 0:16]], alu_op=1)]
-        g.wait_ge(S.arr1, (n - 1) + 8)
+                                srcs=srcs, dsts=[T.land[:, 16 * m:16 + 16 * m]], alu_op=1)]
+        g.wait_ge(S.arr1, (PER - 1) + 8 if own else PER)
         g.remote_dma_fused(tr, local_sem=S.sent)
         g.wait_ge(S.sent, 16)

@@ -36,12 +36,9 @@ def rank_program(g, core, T, topo):
         mid, slot = MID[a // PER], a % PER
         g.sync.dma_start(T.xd[:], T.x[:]).then_inc(S.ld, 16)
         g.vector.memset(T.cst[:], 1.0 / len(T.cores)).then_inc(S.c_ok, 1)
-        tr = []
-        for d in range(1, n):
-            tr.append(RemoteDMATransfer(dst_ids=[dst(plane[(a + d) % n] * 8 + mid)], dma_engine_mask=1 << (d - 1),
-                                        remote_sem=S.arr1, srcs=[T.xd[:]], dsts=[T.gath[slot]], alu_op=0))
-        tr.append(RemoteDMATransfer(dst_ids=[dst(ch * 8 + mid)], dma_engine_mask=0xFF00,
-                                    remote_sem=S.arr1, srcs=[T.xd[:]], dsts=[T.gath[slot]], alu_op=0))
+        order = [plane[(a + d) % n] for d in range(1, n + 1)]
+        tr = [RemoteDMATransfer(dst_ids=[dst(c * 8 + mid) for c in order], dma_engine_mask=0x00FF, remote_sem=S.arr1,
+                                srcs=[T.xd[:]], dsts=[T.gath[slot] for c in order], alu_op=0)]
         g.wait_ge(S.ld, 16)
         g.remote_dma_fused(tr, local_sem=S.sent)
         v = g.vector
@@ -58,17 +55,16 @@ def rank_program(g, core, T, topo):
         g.sync.wait_ge(S.o_ok, 1)
         g.sync.dma_start(T.y[:], T.out[:, 0:1]).then_inc(S.st, 16)
         g.sync.wait_ge(S.st, 16)
-        g.wait_ge(S.sent, (n - 1) + 8)
+        g.wait_ge(S.sent, 8)
         return
 
     if k in MID and ch in rank_on and (ch ^ 1) in rank_on:
         m = MID.index(k)
-        own = plane.index(ch) // PER == m
         srcs = [T.gath[s] for s in range(PER)]
         tr = [RemoteDMATransfer(dst_ids=[dst(rank_on[ch ^ 1])], dma_engine_mask=0x00FF, remote_sem=S.arr2,
                                 srcs=srcs, dsts=[T.land[:, 64 + 16 * m:80 + 16 * m]], alu_op=1),
               RemoteDMATransfer(dst_ids=[dst(rank_on[ch])], dma_engine_mask=0xFF00, remote_sem=S.arr2,
                                 srcs=srcs, dsts=[T.land[:, 16 * m:16 + 16 * m]], alu_op=1)]
-        g.wait_ge(S.arr1, (PER - 1) + 8 if own else PER)
+        g.wait_ge(S.arr1, 8 * PER)
         g.remote_dma_fused(tr, local_sem=S.sent)
         g.wait_ge(S.sent, 16)

from concourse.bass import DstId, RemoteDMATransfer
from concourse.mybir import AluOpType

SCRATCH = {
    "land": ("sbuf", [128, 128], "float32"),
    "cst": ("sbuf", [128, 4], "float32"),
    "t4": ("sbuf", [128, 4], "float32"),
    "t2": ("sbuf", [128, 4], "float32"),
    "t1": ("sbuf", [128, 4], "float32"),
    "out": ("sbuf", [128, 4], "float32"),
    "xd": ("dram", [128, 16], "float32"),
    "gath": ("dram", [2, 128, 16], "float32"),
}
SEMAPHORES = ["ld", "sent", "arr1", "arr2", "c_ok", "t4_ok", "t2_ok", "t1_ok", "o_ok", "st"]

MID = [6, 7, 2, 3]
PER = 2


def rank_program(g, core, T, topo):
    S = T.sem
    ch, k = topo.chip(core), core % 8
    rank_on = {}
    for c in T.cores:
        rank_on[topo.chip(c)] = c
    plane = sorted(c for c in rank_on if (c & 1) == (ch & 1))
    n = len(plane)

    def dst(c):
        rid, pid, _se = topo.addr(c)
        return DstId(rid=rid, pnc=pid)

    rank = T.rank_of(core)
    if rank is not None:
        a = plane.index(ch)
        mid, slot = MID[a // PER], a % PER
        g.sync.dma_start(T.xd[:], T.x[:]).then_inc(S.ld, 16)
        g.vector.memset(T.cst[:], 1.0 / len(T.cores)).then_inc(S.c_ok, 1)
        order = [plane[(a + d) % n] for d in range(1, n + 1)]
        tr = [RemoteDMATransfer(dst_ids=[dst(c * 8 + mid) for c in order], dma_engine_mask=0x00FF, remote_sem=S.arr1,
                                srcs=[T.xd[:]], dsts=[T.gath[slot] for c in order], alu_op=0)]
        g.wait_ge(S.ld, 16)
        g.remote_dma_fused(tr, local_sem=S.sent)
        v = g.vector
        r = rank
        v.wait_ge(S.c_ok, 1)
        v.wait_ge(S.arr2, 8 * 2 * len(MID))
        v.tensor_tensor(T.t4[:, 0:4], T.land[:, r:64:16], T.land[:, 64 + r:128:16], AluOpType.add).then_inc(S.t4_ok, 1)
        v.wait_ge(S.t4_ok, 1)
        v.tensor_tensor(T.t2[:, 0:2], T.t4[:, 0:2], T.t4[:, 2:4], AluOpType.add).then_inc(S.t2_ok, 1)
        v.wait_ge(S.t2_ok, 1)
        v.tensor_tensor(T.t1[:, 0:1], T.t2[:, 0:1], T.t2[:, 1:2], AluOpType.add).then_inc(S.t1_ok, 1)
        v.wait_ge(S.t1_ok, 1)
        v.tensor_tensor(T.out[:, 0:1], T.t1[:, 0:1], T.cst[:, 0:1], AluOpType.mult).then_inc(S.o_ok, 1)
        g.sync.wait_ge(S.o_ok, 1)
        g.sync.dma_start(T.y[:], T.out[:, 0:1]).then_inc(S.st, 16)
        g.sync.wait_ge(S.st, 16)
        g.wait_ge(S.sent, 8)
        return

    if k in MID and ch in rank_on and (ch ^ 1) in rank_on:
        m = MID.index(k)
        srcs = [T.gath[s] for s in range(PER)]
        tr = [RemoteDMATransfer(dst_ids=[dst(rank_on[ch ^ 1])], dma_engine_mask=0x00FF, remote_sem=S.arr2,
                                srcs=srcs, dsts=[T.land[:, 64 + 16 * m:80 + 16 * m]], alu_op=1),
              RemoteDMATransfer(dst_ids=[dst(rank_on[ch])], dma_engine_mask=0xFF00, remote_sem=S.arr2,
                                srcs=srcs, dsts=[T.land[:, 16 * m:16 + 16 * m]], alu_op=1)]
        g.wait_ge(S.arr1, 8 * PER)
        g.remote_dma_fused(tr, local_sem=S.sent)
        g.wait_ge(S.sent, 16)
